import numpy as np
import ml_dtypes


def mxq(x, axis, fmt="e4m3"):
    dtype, down = {"e4m3": (ml_dtypes.float8_e4m3fn, 7), "e5m2": (ml_dtypes.float8_e5m2, 14)}[fmt]
    v = np.moveaxis(np.asarray(x, np.float32).astype(ml_dtypes.bfloat16).astype(np.float64), axis, -1)
    blocks = v.reshape(v.shape[:-1] + (-1, 32))
    amax = np.abs(blocks).max(-1, keepdims=True)
    byte = np.maximum(np.where(amax > 0, np.frexp(amax)[1] - 1 + 127, 0) - down, 1)
    scale = np.exp2(byte - 127.0)
    codes = (blocks / scale).astype(np.float32).astype(dtype).astype(np.float64)
    return np.moveaxis((codes * scale).reshape(v.shape), -1, axis)


WIDE = False


def mx_kscale(k):
    if not WIDE:
        return np.ones(k)
    levels = np.array([10, -10, 5, -5, 0])
    if k % 512:
        return np.exp2(np.random.permutation(np.resize(levels, k // 32))).repeat(32)
    a = np.empty((k // 512, 16))
    for p in range(k // 512):
        a[p, :8] = np.random.permutation(np.resize(levels, 8))
        for g in range(8):
            far = levels[np.abs(levels - a[p, g]) >= 10]
            a[p, g + 8] = far[np.random.randint(len(far))]
    return np.exp2(a.ravel()).repeat(32)


def f64(x):
    return np.asarray(x).astype(np.float64)


def striped(idx):
    return np.tile(idx.reshape(-1, 16).T, (8, 1)).astype(np.uint16)


def unstriped(offs):
    return offs[:16].T.reshape(-1).astype(np.int64)


def striped8(idx):
    return np.concatenate([x.reshape(-1, 16).T for x in idx]).astype(np.uint16)


def runs(offs, k):
    lists = np.stack([offs[16 * r : 16 * r + 16].T.reshape(-1) for r in range(8)]).astype(np.int64)
    return lists[np.arange(k) % 512 // 64]


def pack_weight(w):
    k, n = w.shape
    w = f64(np.asarray(w, np.float32).astype(ml_dtypes.bfloat16)).reshape(k // 32, 32, n)
    amax = np.abs(w).max(1)
    byte = np.clip(np.where(amax > 0, np.frexp(amax)[1] - 1 + 127 - 7, 1), 1, 254)
    scaled = (w * np.exp2(127.0 - byte)[:, None, :]).reshape(k, n).astype(np.float32)
    words = np.ascontiguousarray(scaled.reshape(k // 512, 128, 4, n).transpose(0, 1, 3, 2)).astype(ml_dtypes.float8_e4m3fn).view(np.uint8)
    return words, np.ascontiguousarray(byte.astype(np.uint8).reshape(k // 512, 16, n))


def unpack_weight(words, scales):
    g, p, n, _ = words.shape
    vals = np.ascontiguousarray(words).view(ml_dtypes.float8_e4m3fn).astype(np.float64) * np.repeat(np.exp2(scales.astype(np.float64) - 127.0), 8, axis=1)[..., None]
    return vals.transpose(0, 1, 3, 2).reshape(g * 512, n)

def planes(y):
    n, m = y.shape
    v = y.astype(np.float32).astype(ml_dtypes.bfloat16).astype(np.float64).reshape(n // 32, 32, m)
    top = np.abs(v).max(1)
    byte = np.clip(np.where(top > 0, np.frexp(top)[1] - 1 + 127 - 7, 1), 1, 254)
    codes = (v * np.exp2(127.0 - byte)[:, None, :]).reshape(n, m).astype(np.float32).astype(ml_dtypes.float8_e4m3fn).view(np.uint8)
    words = codes.reshape(n // 512, 128, 4, m).transpose(0, 1, 3, 2)
    return np.ascontiguousarray(words), np.ascontiguousarray(byte.astype(np.uint8).reshape(n // 512, 16, m))


K, T, S, N, H = 512, 2048, 512, 512, 512


def setup_inputs():
    n = np.random.standard_normal
    s = mx_kscale(K)[:, None]
    u = mx_kscale(S)
    packed_xT = pack_weight(n((K, T)) * s)
    packed_w1 = pack_weight(n((S, N)) / np.sqrt(S) / u[:, None])
    return {
        "x_words": packed_xT[0],
        "x_scales": packed_xT[1],
        "wa": (n((K, H)) / np.sqrt(K) / s).astype(np.float32),
        "gt": (np.random.uniform(0.5, 1.5, (S, 1)) * u[:, None]).astype(np.float32),
        "w1_words": packed_w1[0],
        "w1_scales": packed_w1[1],
        "offs": striped(np.random.permutation(T)[:S]),
        "n1": striped8(np.stack([np.random.permutation(H) for _ in range(8)])),
        "n2": striped8(np.stack([np.random.permutation(H) for _ in range(8)])),
        "n3": striped8(np.stack([np.random.permutation(H) for _ in range(8)])),
    }


def reference(x_words, x_scales, wa, gt, w1_words, w1_scales, offs, n1, n2, n3):
    xq = unpack_weight(x_words, x_scales)[:, unstriped(offs)]
    y = xq.T @ mxq(f64(wa), 0, "e4m3")
    pa = y[np.arange(S)[:, None], runs(n1, S)]
    pb = y[np.arange(S)[:, None], runs(n2, S)]
    mu = 0.3125 * (y + pa + pb)
    z = f64(gt) * ((y - mu) / (np.sqrt((pa - mu) ** 2 + (pb - mu) ** 2 + 0.25)))
    h = unpack_weight(w1_words, w1_scales).T @ mxq(z, 0, "e4m3")
    st = h - (h[np.arange(N)[:, None], runs(n3, N)])
    out_0 = st - (0.5 * (st[np.arange(N)[:, None], runs(n3, N)]))
    return (out_0,) + planes(out_0)

@@ -1,0 +1,302 @@
+from contextlib import ExitStack
+
+import concourse.mybir as mybir
+from concourse.masks import make_identity
+
+K, T, S, N, H = 512, 2048, 512, 512, 512
+FLOPS = 2 * K * S * H + 2 * S * N * H
+
+F32 = mybir.dt.float32
+BF16 = mybir.dt.bfloat16
+I32 = mybir.dt.int32
+U32 = mybir.dt.uint32
+U16 = mybir.dt.uint16
+U8 = mybir.dt.uint8
+FP8X4 = mybir.dt.float8_e4m3fn_x4
+ALU = mybir.AluOpType
+ACT = mybir.ActivationFunctionType
+
+P = 128
+
+CH = [(0, 256), (256, 384), (384, 512)]
+
+
+def tile_picked_tokstdtwice_none_po_kernel(
+    tc, x_words, x_scales, wa, gt, w1_words, w1_scales, offs, n1, n2, n3, out_0, out_1, out_2
+):
+    nc = tc.nc
+    with ExitStack() as ctx:
+        sb = ctx.enter_context(tc.tile_pool(name="sb", bufs=1))
+        ps = ctx.enter_context(tc.psum_pool(name="ps", bufs=1))
+
+        def tl(name, shape, dt, tag=None):
+            return sb.tile(shape, dt, name=name, tag=tag or name, align_bytes=64)
+
+        def lst(lt, a, b):
+            return lt[:, a // 16 : b // 16]
+
+        xs = tl("xs", [P, T], U8)
+        nc.vector.memset(xs[:].bitcast(I32), 0)
+        w1s = tl("w1s", [P, N], U8)
+        nc.vector.memset(w1s[:].bitcast(I32), 0)
+        sixteen = tl("sixteen", [P, 1], F32)
+        nc.gpsimd.memset(sixteen[:], 16.0)
+        quarter = tl("quarter", [P, 1], F32)
+        nc.scalar.activation(quarter[:], sixteen[:], ACT.Abs_reciprocal_sqrt)
+
+        ident = tl("ident", [P, P], F32)
+        make_identity(nc, ident[:])
+
+        offs_t = tl("offs_t", [P, S // 16], U16)
+        n1_t = tl("n1_t", [P, H // 16], U16)
+        n2_t = tl("n2_t", [P, H // 16], U16)
+        n3_t = tl("n3_t", [P, H // 16], U16)
+        for lt, src in ((offs_t, offs), (n1_t, n1), (n2_t, n2), (n3_t, n3)):
+            nc.sync.dma_start(lt[:], src)
+        xw = tl("xw", [P, T], U32)
+        nc.sync.dma_start(xw[:].bitcast(I32), x_words[0].rearrange("p n t -> p (n t)").bitcast(I32))
+        for q in range(4):
+            nc.sync.dma_start(xs[32 * q : 32 * q + 4, :].bitcast(I32), x_scales[0, 4 * q : 4 * q + 4, :].bitcast(I32))
+        wa_v = wa.rearrange("(p j) h -> p j h", j=4)
+        wraw = []
+        for c, (a, b) in enumerate(CH):
+            w = tl(f"wraw{c}", [P, 4, b - a], F32)
+            nc.sync.dma_start(w[:], wa_v[:, :, a:b])
+            wraw.append(w)
+        gt_t = tl("gt_t", [P, 4], F32)
+        nc.sync.dma_start(gt_t[:], gt.rearrange("(p t) o -> p (t o)", t=4))
+        w1w = tl("w1w", [P, N], U32)
+        nc.sync.dma_start(w1w[:].bitcast(I32), w1_words[0].rearrange("p n t -> p (n t)").bitcast(I32))
+        for q in range(4):
+            nc.sync.dma_start(w1s[32 * q : 32 * q + 4, :].bitcast(I32), w1_scales[0, 4 * q : 4 * q + 4, :].bitcast(I32))
+
+        def deal(name, words, scales, tags=(None, None)):
+            dw = tl(name + "_dw", [P, 512], U32, tag=tags[0])
+            ds = tl(name + "_ds", [P, 512], U8, tag=tags[1])
+            nc.vector.tensor_copy(
+                ds[:].rearrange("p (t c i) -> p c t i", t=4, i=16),
+                scales[:].rearrange("p (c i t) -> p c t i", t=4, i=16),
+            )
+            nc.vector.tensor_copy(
+                dw[:].bitcast(I32).rearrange("p (t c i) -> p c t i", t=4, i=4),
+                words[:].bitcast(I32).rearrange("p (c i t) -> p c t i", t=4, i=4),
+            )
+            return dw, ds
+
+        xsg = tl("xsg", [P, S], U8)
+        nc.vector.tensor_copy(xsg[:], xs[:].indirect(offs_t[:]))
+        xwg = tl("xwg", [P, S], U32)
+        nc.vector.tensor_copy(xwg[:], xw[:].indirect(offs_t[:]))
+        xd, xds = deal("x", xwg, xsg)
+
+        def interleave(eng, dst, src):
+            o = dst[:].rearrange("p (c i) t -> p c t i", i=4)
+            s = src.rearrange("p t (c i) -> p c t i", i=4)
+            if eng == "v":
+                nc.vector.tensor_copy(o, s)
+            else:
+                nc.scalar.copy(o, s)
+
+        def quant(words, scales, src, a, b):
+            nc.vector.quantize_mx(
+                out=words[:, a:b].bitcast(FP8X4), scales=scales[:, a:b], in_=src[:].rearrange("p c t -> p (c t)")
+            )
+
+        def mm(out, lw, ls, t, rw, rs, a, b):
+            nc.tensor.matmul_mx(
+                out=out,
+                lhsT=lw[:, P * t : P * (t + 1)].bitcast(FP8X4),
+                lhsT_scale=ls[:, P * t : P * (t + 1)],
+                rhs=rw[:, a:b].bitcast(FP8X4),
+                rhs_scale=rs[:, a:b],
+                start=True,
+                stop=True,
+            )
+
+        gtc = tl("gtc", [P, 4], F32)
+        nc.vector.tensor_scalar(gtc[:], gt_t[:], -0.3125, None, ALU.mult)
+
+        waq = tl("waq", [P, H], U32)
+        was = tl("was", [P, H], U8)
+        ya = [ps.tile([P, 512], F32, name=f"ya{t}", tag=f"b{t}") for t in range(4)]
+        yb = [ps.tile([P, 512], F32, name=f"yb{t}", tag=f"b{4 + t}") for t in range(4)]
+        for c, (a, b) in enumerate(CH):
+            wb = tl(f"wb{c}", [P, b - a, 4], BF16)
+            interleave("s" if c < 2 else "v", wb, wraw[c][:])
+            quant(waq, was, wb, a, b)
+        for t in range(4):
+            for c, (a, b) in enumerate(CH):
+                bank = ya[t] if c < 2 else yb[t]
+                mm(bank[:, a:b], xd, xds, t, waq, was, a, b)
+        w1d, w1ds = deal("w1", w1w, w1s)
+        gt6 = tl("gt6", [P, 4], F32)
+        nc.vector.tensor_scalar(gt6[:], gt_t[:], 1.0 / 6.0, None, ALU.mult)
+
+        M = 384
+        ywin = [tl(f"ywin{t}", [P, H], F32) for t in range(4)]
+        yk = tl("yk", [P, 4, H], F32)
+        yg = tl("yg", [P, 4, H], F32)
+        A = tl("A", [P, 4, M], F32)
+        U = tl("U", [P, 4, H], F32)
+        Eg = tl("Eg", [P, 4, H], F32)
+        R = tl("R", [P, 4, H], F32)
+        zq = tl("zq", [P, H], U32)
+        zs = tl("zs", [P, H], U8)
+        hwin = [tl(f"hwin{t}", [P, H], F32) for t in range(4)]
+        hpl = tl("hpl", [P, 4, H], F32)
+
+        def windows(t):
+            nc.scalar.copy(ywin[t][:, 0:M], ya[t][:, 0:M])
+            nc.scalar.copy(ywin[t][:, M:H], yb[t][:, M:H])
+            if t == 0:
+                nc.vector.tensor_scalar(yk[:, t, 0:M], ywin[t][:, 0:M], -5.0 / 3.0, None, ALU.mult)
+                nc.scalar.activation(yk[:, t, M:H], ywin[t][:, M:H], ACT.Copy, scale=-5.0 / 3.0)
+            else:
+                nc.scalar.activation(yk[:, t, :], ywin[t][:], ACT.Copy, scale=-5.0 / 3.0)
+
+        def ygate(t, eng):
+            if eng == "s":
+                nc.scalar.activation(yg[:, t, :], ywin[t][:], ACT.Copy, scale=gt6[:, t : t + 1])
+            else:
+                nc.vector.tensor_scalar(yg[:, t, :], ywin[t][:], gt6[:, t : t + 1], None, ALU.mult)
+
+        def g1(t, a, b, dst):
+            nc.vector.tensor_tensor(dst, ywin[t][:].indirect(lst(n1_t, a, b)), yk[:, t, a:b], ALU.add)
+
+        def g2(t, a, b, k):
+            nc.vector.tensor_tensor(U[:, t, a:b], ywin[t][:].indirect(lst(n2_t, a, b)), k, ALU.add)
+
+        def tadd(out, terms):
+            for i, x in enumerate(terms):
+                nc.tensor.matmul(out, lhsT=x, rhs=ident[:], is_transpose=True, start=(i == 0), stop=(i == len(terms) - 1))
+
+        st = {}
+
+        def squares(n, a, u, k, nb):
+            X = tl(f"X{n}", [P, nb, P], F32)
+            nc.vector.scalar_tensor_tensor(X[:], a, -2.0, u, ALU.mult, ALU.add)
+            ut = ps.tile([P, nb, P], F32, name=f"ut{n}", tag=f"b{(4, 5, 6, 7, 6, 7)[n]}")
+            vt = ps.tile([P, nb, P], F32, name=f"vt{n}", tag=f"b{(0, 1, 2, 3, 3, 6)[n]}")
+            for j in range(nb):
+                tadd(ut[:, j, :], [u[:, j, :]])
+            for j in range(nb):
+                tadd(vt[:, j, :], [X[:, j, :], k[:, j, :]])
+            U2 = tl(f"U2{n}", [P, nb, P], F32)
+            V2 = tl(f"V2{n}", [P, nb, P], F32)
+            nc.scalar.activation(U2[:], ut[:], ACT.Square, scale=0.375)
+            nc.scalar.activation(V2[:], vt[:], ACT.Square)
+            st[n] = (U2, V2, nb)
+
+        def root(n, dst):
+            U2, V2, nb = st[n]
+            d = ps.tile([P, nb, P], F32, name=f"d{n}", tag=f"b{(4, 5, 6, 7, 0, 1)[n]}")
+            for j in range(nb):
+                tadd(d[:, j, :], [V2[:, j, :], U2[:, j, :]])
+            nc.scalar.activation(dst, d[:], ACT.Abs_reciprocal_sqrt, scale=0.5, bias=quarter[:])
+
+        def blocks(ap):
+            return ap.rearrange("p (j f) -> p j f", f=P)
+
+        def finish(a, b):
+            zb = tl(f"zb{a}", [P, b - a, 4], BF16)
+            nc.vector.tensor_tensor(
+                zb[:].rearrange("p (c i) t -> p c t i", i=4),
+                Eg[:, :, a:b].rearrange("p t (c i) -> p c t i", i=4),
+                R[:, :, a:b].rearrange("p t (c i) -> p c t i", i=4),
+                ALU.mult,
+            )
+            return zb
+
+        def gate(t, a, b):
+            nc.vector.scalar_tensor_tensor(Eg[:, t, a:b], U[:, t, a:b], gtc[:, t : t + 1], yg[:, t, a:b], ALU.mult, ALU.add)
+
+        windows(0)
+        windows(1)
+        for t in range(4):
+            g1(t, 0, 256, A[:, t, 0:256])
+            g1(t, 256, M, A[:, t, 256:M])
+            g2(t, 0, 256, A[:, t, 0:256])
+            g2(t, 256, M, A[:, t, 256:M])
+            if t + 2 < 4:
+                windows(t + 2)
+            squares(t, blocks(A[:, t, :]), blocks(U[:, t, 0:M]), blocks(yk[:, t, 0:M]), 3)
+            if t > 0:
+                root(t - 1, blocks(R[:, t - 1, 0:M]))
+            ygate(t, "sssv"[t])
+
+        Al = tl("Al", [P, 4, P], F32, tag="X2")
+        groups = [(0, 2), (2, 4)]
+        g1(0, M, H, Al[:, 0, :])
+        for t in range(4):
+            if t < 3:
+                g1(t + 1, M, H, Al[:, t + 1, :])
+            g2(t, M, H, Al[:, t, :])
+            if t == 0:
+                root(3, blocks(R[:, 3, 0:M]))
+            for u, (ta, tb) in enumerate(groups):
+                if t == tb - 1:
+                    squares(4 + u, Al[:, ta:tb, :], U[:, ta:tb, M:H], yk[:, ta:tb, M:H], tb - ta)
+                    if u > 0:
+                        root(3 + u, R[:, groups[u - 1][0] : groups[u - 1][1], M:H])
+        root(3 + len(groups), R[:, groups[-1][0] : groups[-1][1], M:H])
+        for t in range(4):
+            gate(t, 0, H)
+        ha = ps.tile([P, M], F32, name="ha", tag="b2")
+        hb = ps.tile([P, P], F32, name="hb", tag="b4")
+        zb0 = finish(0, 256)
+        zb1 = finish(256, M)
+        quant(zq, zs, zb0, 0, 256)
+        quant(zq, zs, zb1, 256, M)
+        mm(ha[:, 0:256], w1d, w1ds, 0, zq, zs, 0, 256)
+        mm(ha[:, 256:M], w1d, w1ds, 0, zq, zs, 256, M)
+        zb2 = finish(M, H)
+        quant(zq, zs, zb2, M, H)
+        mm(hb[:], w1d, w1ds, 0, zq, zs, M, H)
+        hs = [None] + [ps.tile([P, H], F32, name=f"h{t}", tag=f"b{(0, 5, 3, 0)[t]}") for t in range(1, 4)]
+        for t in range(1, 4):
+            mm(hs[t][:], w1d, w1ds, t, zq, zs, 0, H)
+
+        swin = [tl(f"swin{t}", [P, H], F32) for t in range(4)]
+        spl = tl("spl", [P, 4, H], F32)
+
+        def hcopies(t):
+            if t == 0:
+                nc.scalar.activation(hwin[t][:, 0:M], ha[:], ACT.Copy, scale=0.5)
+                nc.scalar.activation(hpl[:, t, 0:M], ha[:], ACT.Copy, scale=0.5)
+                nc.scalar.activation(hwin[t][:, M:H], hb[:], ACT.Copy, scale=0.5)
+                nc.scalar.activation(hpl[:, t, M:H], hb[:], ACT.Copy, scale=0.5)
+            else:
+                nc.scalar.activation(hwin[t][:], hs[t][:], ACT.Copy, scale=0.5)
+                nc.scalar.activation(hpl[:, t, 0:256], hs[t][:, 0:256], ACT.Copy, scale=0.5)
+                nc.scalar.activation(hpl[:, t, 256:H], hs[t][:, 256:H], ACT.Copy, scale=0.5)
+
+        hcopies(0)
+        hcopies(1)
+        for t in range(4):
+            for a, b in ((0, 256), (256, 512)):
+                nc.vector.tensor_tensor(swin[t][:, a:b], hwin[t][:].indirect(lst(n3_t, a, b)), hpl[:, t, a:b], ALU.subtract)
+            if t + 2 < 4:
+                hcopies(t + 2)
+        for a, b in ((0, 256), (256, 512)):
+            for t in range(4):
+                nc.scalar.activation(spl[:, t, a:b], swin[t][:, a:b], ACT.Copy, scale=2.0)
+
+        oq = tl("oq", [P, H], U32)
+        osc = tl("osc", [P, H], U8)
+        out_v = out_0.rearrange("(p t) h -> p t h", t=4)
+        words_v = out_1[0].rearrange("p n t -> p (n t)").bitcast(I32)
+        obs = []
+        for c, (a, b) in enumerate(CH):
+            O = tl(f"O{c}", [P, 4, b - a], F32)
+            for t in range(4):
+                nc.vector.tensor_tensor(O[:, t, :], swin[t][:].indirect(lst(n3_t, a, b)), spl[:, t, a:b], ALU.subtract)
+            nc.sync.dma_start(out_v[:, :, a:b], O[:])
+            ob = tl(f"ob{c}", [P, b - a, 4], BF16)
+            interleave("s" if c < 2 else "v", ob, O[:])
+            obs.append(ob)
+        for c, (a, b) in enumerate(CH):
+            quant(oq, osc, obs[c], a, b)
+            nc.sync.dma_start(words_v[:, a:b], oq[:, a:b].bitcast(I32))
+        for q in range(4):
+            eng = nc.scalar if q % 2 == 0 else nc.sync
+            eng.dma_start(out_2[0, 4 * q : 4 * q + 4, :].bitcast(I32), osc[32 * q : 32 * q + 4, :].bitcast(I32))

@@ -70,24 +70,23 @@ def tile_picked_tokstdtwice_none_po_kernel(
         for q in range(4):
             nc.sync.dma_start(w1s[32 * q : 32 * q + 4, :].bitcast(I32), w1_scales[0, 4 * q : 4 * q + 4, :].bitcast(I32))
 
-        def deal(name, words, scales, tags=(None, None)):
-            dw = tl(name + "_dw", [P, 512], U32, tag=tags[0])
-            ds = tl(name + "_ds", [P, 512], U8, tag=tags[1])
+        def deal(dw, ds, words, scales, ta, tb):
             nc.vector.tensor_copy(
-                ds[:].rearrange("p (t c i) -> p c t i", t=4, i=16),
-                scales[:].rearrange("p (c i t) -> p c t i", t=4, i=16),
+                dw[:].bitcast(I32).rearrange("p (t c i) -> p c t i", t=4, i=4)[:, :, ta:tb, :],
+                words[:].bitcast(I32).rearrange("p (c i t) -> p c t i", t=4, i=4)[:, :, ta:tb, :],
             )
             nc.vector.tensor_copy(
-                dw[:].bitcast(I32).rearrange("p (t c i) -> p c t i", t=4, i=4),
-                words[:].bitcast(I32).rearrange("p (c i t) -> p c t i", t=4, i=4),
+                ds[:].rearrange("p (t c i) -> p c t i", t=4, i=16)[:, :, ta:tb, :],
+                scales[:].rearrange("p (c i t) -> p c t i", t=4, i=16)[:, :, ta:tb, :],
             )
-            return dw, ds
 
-        xsg = tl("xsg", [P, S], U8)
-        nc.vector.tensor_copy(xsg[:], xs[:].indirect(offs_t[:]))
         xwg = tl("xwg", [P, S], U32)
         nc.vector.tensor_copy(xwg[:], xw[:].indirect(offs_t[:]))
-        xd, xds = deal("x", xwg, xsg)
+        xsg = tl("xsg", [P, S], U8)
+        nc.vector.tensor_copy(xsg[:], xs[:].indirect(offs_t[:]))
+        xd = tl("xd", [P, S], U32)
+        xds = tl("xds", [P, S], U8)
+        deal(xd, xds, xwg, xsg, 0, 1)
 
         def interleave(eng, dst, src):
             o = dst[:].rearrange("p (c i) t -> p c t i", i=4)
@@ -114,29 +113,33 @@ def tile_picked_tokstdtwice_none_po_kernel(
             )
 
         gtc = tl("gtc", [P, 4], F32)
-        nc.vector.tensor_scalar(gtc[:], gt_t[:], -0.3125, None, ALU.mult)
+        nc.gpsimd.tensor_scalar(gtc[:], gt_t[:], -0.3125, 0.0, ALU.mult, ALU.add)
 
         waq = tl("waq", [P, H], U32)
         was = tl("was", [P, H], U8)
-        ya = [ps.tile([P, 512], F32, name=f"ya{t}", tag=f"b{t}") for t in range(4)]
-        yb = [ps.tile([P, 512], F32, name=f"yb{t}", tag=f"b{4 + t}") for t in range(4)]
+        y0 = [ps.tile([P, b - a], F32, name=f"y0{c}", tag=f"b{(0, 4, 5)[c]}") for c, (a, b) in enumerate(CH)]
+        ys = [None] + [ps.tile([P, H], F32, name=f"y{t}", tag=f"b{t}") for t in range(1, 4)]
         for c, (a, b) in enumerate(CH):
             wb = tl(f"wb{c}", [P, b - a, 4], BF16)
-            interleave("s" if c < 2 else "v", wb, wraw[c][:])
+            interleave("sss"[c], wb, wraw[c][:])
             quant(waq, was, wb, a, b)
-        for t in range(4):
-            for c, (a, b) in enumerate(CH):
-                bank = ya[t] if c < 2 else yb[t]
-                mm(bank[:, a:b], xd, xds, t, waq, was, a, b)
-        w1d, w1ds = deal("w1", w1w, w1s)
+            mm(y0[c][:], xd, xds, 0, waq, was, a, b)
+        deal(xd, xds, xwg, xsg, 1, 2)
+        deal(xd, xds, xwg, xsg, 2, 4)
+        for t in range(1, 4):
+            mm(ys[t][:], xd, xds, t, waq, was, 0, H)
+        w1d = tl("w1d", [P, N], U32, tag=None)
+        w1ds = tl("w1ds", [P, N], U8)
         gt6 = tl("gt6", [P, 4], F32)
-        nc.vector.tensor_scalar(gt6[:], gt_t[:], 1.0 / 6.0, None, ALU.mult)
+        nc.gpsimd.tensor_scalar(gt6[:], gt_t[:], 1.0 / 6.0, 0.0, ALU.mult, ALU.add)
+        FORM = "WWWWW"
+        KS = {"T": -2.2, "W": -5.0 / 3.0}
 
         M = 384
         ywin = [tl(f"ywin{t}", [P, H], F32) for t in range(4)]
         yk = tl("yk", [P, 4, H], F32)
         yg = tl("yg", [P, 4, H], F32)
-        A = tl("A", [P, 4, M], F32)
+        A = [tl(f"A{t}", [P, M], F32) for t in range(4)]
         U = tl("U", [P, 4, H], F32)
         Eg = tl("Eg", [P, 4, H], F32)
         R = tl("R", [P, 4, H], F32)
@@ -146,19 +149,31 @@ def tile_picked_tokstdtwice_none_po_kernel(
         hpl = tl("hpl", [P, 4, H], F32)
 
         def windows(t):
-            nc.scalar.copy(ywin[t][:, 0:M], ya[t][:, 0:M])
-            nc.scalar.copy(ywin[t][:, M:H], yb[t][:, M:H])
             if t == 0:
-                nc.vector.tensor_scalar(yk[:, t, 0:M], ywin[t][:, 0:M], -5.0 / 3.0, None, ALU.mult)
-                nc.scalar.activation(yk[:, t, M:H], ywin[t][:, M:H], ACT.Copy, scale=-5.0 / 3.0)
+                for c, (a, b) in enumerate(CH):
+                    nc.scalar.copy(ywin[t][:, a:b], y0[c][:])
+                    if c < 2:
+                        nc.vector.tensor_scalar(yk[:, t, a:b], ywin[t][:, a:b], KS[FORM[t]], None, ALU.mult)
+                nc.scalar.activation(yk[:, t, M:H], y0[2][:], ACT.Copy, scale=KS[FORM[4]])
             else:
-                nc.scalar.activation(yk[:, t, :], ywin[t][:], ACT.Copy, scale=-5.0 / 3.0)
+                nc.scalar.copy(ywin[t][:], ys[t][:])
+                if FORM[t] == FORM[4]:
+                    nc.scalar.activation(yk[:, t, :], ys[t][:], ACT.Copy, scale=KS[FORM[t]])
+                else:
+                    nc.scalar.activation(yk[:, t, 0:M], ys[t][:, 0:M], ACT.Copy, scale=KS[FORM[t]])
+                    nc.scalar.activation(yk[:, t, M:H], ys[t][:, M:H], ACT.Copy, scale=KS[FORM[4]])
 
-        def ygate(t, eng):
+        def scaled(eng, dst, src, scale):
             if eng == "s":
-                nc.scalar.activation(yg[:, t, :], ywin[t][:], ACT.Copy, scale=gt6[:, t : t + 1])
+                nc.scalar.activation(dst, src, ACT.Copy, scale=scale)
             else:
-                nc.vector.tensor_scalar(yg[:, t, :], ywin[t][:], gt6[:, t : t + 1], None, ALU.mult)
+                nc.vector.tensor_scalar(dst, src, scale, None, ALU.mult)
+
+        def aux(t, a, b, form, eng):
+            if form == "W":
+                scaled(eng, yg[:, t, a:b], ywin[t][:, a:b], gt6[:, t : t + 1])
+            else:
+                scaled(eng, yg[:, t, a:b], ywin[t][:, a:b], 8.0 / 15.0)
 
         def g1(t, a, b, dst):
             nc.vector.tensor_tensor(dst, ywin[t][:].indirect(lst(n1_t, a, b)), yk[:, t, a:b], ALU.add)
@@ -172,13 +187,13 @@ def tile_picked_tokstdtwice_none_po_kernel(
 
         st = {}
 
-        def squares(n, a, u, k, nb):
+        def squares(n, a, u, k, k4, nb, form):
             X = tl(f"X{n}", [P, nb, P], F32)
             nc.vector.scalar_tensor_tensor(X[:], a, -2.0, u, ALU.mult, ALU.add)
-            ut = ps.tile([P, nb, P], F32, name=f"ut{n}", tag=f"b{(4, 5, 6, 7, 6, 7)[n]}")
-            vt = ps.tile([P, nb, P], F32, name=f"vt{n}", tag=f"b{(0, 1, 2, 3, 3, 6)[n]}")
+            ut = ps.tile([P, nb, P], F32, name=f"ut{n}", tag=f"b{(6, 7, 4, 5, 7, 4)[n]}")
+            vt = ps.tile([P, nb, P], F32, name=f"vt{n}", tag=f"b{(0, 1, 2, 3, 2, 3)[n]}")
             for j in range(nb):
-                tadd(ut[:, j, :], [u[:, j, :]])
+                tadd(ut[:, j, :], [u[:, j, :]] if form == "W" else [u[:, j, :], k4[:, j, :]])
             for j in range(nb):
                 tadd(vt[:, j, :], [X[:, j, :], k[:, j, :]])
             U2 = tl(f"U2{n}", [P, nb, P], F32)
@@ -189,7 +204,7 @@ def tile_picked_tokstdtwice_none_po_kernel(
 
         def root(n, dst):
             U2, V2, nb = st[n]
-            d = ps.tile([P, nb, P], F32, name=f"d{n}", tag=f"b{(4, 5, 6, 7, 0, 1)[n]}")
+            d = ps.tile([P, nb, P], F32, name=f"d{n}", tag=f"b{(6, 7, 4, 5, 0, 1)[n]}")
             for j in range(nb):
                 tadd(d[:, j, :], [V2[:, j, :], U2[:, j, :]])
             nc.scalar.activation(dst, d[:], ACT.Abs_reciprocal_sqrt, scale=0.5, bias=quarter[:])
@@ -207,24 +222,38 @@ def tile_picked_tokstdtwice_none_po_kernel(
             )
             return zb
 
-        def gate(t, a, b):
-            nc.vector.scalar_tensor_tensor(Eg[:, t, a:b], U[:, t, a:b], gtc[:, t : t + 1], yg[:, t, a:b], ALU.mult, ALU.add)
+        def gate(t, a, b, form, eng):
+            if form == "W":
+                nc.vector.scalar_tensor_tensor(Eg[:, t, a:b], U[:, t, a:b], gtc[:, t : t + 1], yg[:, t, a:b], ALU.mult, ALU.add)
+            else:
+                scaled(eng, Eg[:, t, a:b], U[:, t, a:b], gtc[:, t : t + 1])
 
+        deal(w1d, w1ds, w1w, w1s, 0, 4)
         windows(0)
-        windows(1)
+        for t in range(1, 4):
+            windows(t)
         for t in range(4):
-            g1(t, 0, 256, A[:, t, 0:256])
-            g1(t, 256, M, A[:, t, 256:M])
-            g2(t, 0, 256, A[:, t, 0:256])
-            g2(t, 256, M, A[:, t, 256:M])
-            if t + 2 < 4:
-                windows(t + 2)
-            squares(t, blocks(A[:, t, :]), blocks(U[:, t, 0:M]), blocks(yk[:, t, 0:M]), 3)
+            if FORM[t] == "T":
+                aux(t, 0, M, "T", "sssss"[t])
+            g1(t, 0, 256, A[t][:, 0:256])
+            g1(t, 256, M, A[t][:, 256:M])
+            g2(t, 0, 256, A[t][:, 0:256])
+            g2(t, 256, M, A[t][:, 256:M])
+            if 4 <= t + 4 < 4 and t == 0:
+                windows(3)
+            squares(t, blocks(A[t][:]), blocks(U[:, t, 0:M]), blocks(yk[:, t, 0:M]), blocks(yg[:, t, 0:M]), 3, FORM[t])
             if t > 0:
                 root(t - 1, blocks(R[:, t - 1, 0:M]))
-            ygate(t, "sssv"[t])
+            if FORM[t] == "W" and FORM[4] == "W":
+                aux(t, 0, H, "W", "sssss"[t])
+            else:
+                if FORM[t] == "W":
+                    aux(t, 0, M, "W", "sssss"[t])
+                elif "vvvvv"[t] == "s":
+                    gate(t, 0, M, "T", "s")
+                aux(t, M, H, FORM[4], "sssss"[4])
 
-        Al = tl("Al", [P, 4, P], F32, tag="X2")
+        Al = tl("Al", [P, 4, P], F32, tag="A3")
         groups = [(0, 2), (2, 4)]
         g1(0, M, H, Al[:, 0, :])
         for t in range(4):
@@ -235,24 +264,28 @@ def tile_picked_tokstdtwice_none_po_kernel(
                 root(3, blocks(R[:, 3, 0:M]))
             for u, (ta, tb) in enumerate(groups):
                 if t == tb - 1:
-                    squares(4 + u, Al[:, ta:tb, :], U[:, ta:tb, M:H], yk[:, ta:tb, M:H], tb - ta)
+                    squares(4 + u, Al[:, ta:tb, :], U[:, ta:tb, M:H], yk[:, ta:tb, M:H], yg[:, ta:tb, M:H], tb - ta, FORM[4])
                     if u > 0:
                         root(3 + u, R[:, groups[u - 1][0] : groups[u - 1][1], M:H])
         root(3 + len(groups), R[:, groups[-1][0] : groups[-1][1], M:H])
         for t in range(4):
-            gate(t, 0, H)
-        ha = ps.tile([P, M], F32, name="ha", tag="b2")
-        hb = ps.tile([P, P], F32, name="hb", tag="b4")
+            if t >= 4 and FORM[t] == FORM[4] and (FORM[t] == "W" or "vvvvv"[t] == "v"):
+                gate(t, 0, H, FORM[t], "v")
+            else:
+                if FORM[t] == "W" or "vvvvv"[t] == "v":
+                    gate(t, 0, M, FORM[t], "v")
+                gate(t, M, H, FORM[4], "vvvvv"[4])
+        h0 = [ps.tile([P, b - a], F32, name=f"h0{c}", tag=f"b{(2, 6, 4)[c]}") for c, (a, b) in enumerate(CH)]
         zb0 = finish(0, 256)
         zb1 = finish(256, M)
         quant(zq, zs, zb0, 0, 256)
-        quant(zq, zs, zb1, 256, M)
-        mm(ha[:, 0:256], w1d, w1ds, 0, zq, zs, 0, 256)
-        mm(ha[:, 256:M], w1d, w1ds, 0, zq, zs, 256, M)
+        mm(h0[0][:], w1d, w1ds, 0, zq, zs, 0, 256)
         zb2 = finish(M, H)
+        quant(zq, zs, zb1, 256, M)
+        mm(h0[1][:], w1d, w1ds, 0, zq, zs, 256, M)
         quant(zq, zs, zb2, M, H)
-        mm(hb[:], w1d, w1ds, 0, zq, zs, M, H)
-        hs = [None] + [ps.tile([P, H], F32, name=f"h{t}", tag=f"b{(0, 5, 3, 0)[t]}") for t in range(1, 4)]
+        mm(h0[2][:], w1d, w1ds, 0, zq, zs, M, H)
+        hs = [None] + [ps.tile([P, H], F32, name=f"h{t}", tag=f"b{(0, 7, 3, 5)[t]}") for t in range(1, 4)]
         for t in range(1, 4):
             mm(hs[t][:], w1d, w1ds, t, zq, zs, 0, H)
 
@@ -261,10 +294,12 @@ def tile_picked_tokstdtwice_none_po_kernel(
 
         def hcopies(t):
             if t == 0:
-                nc.scalar.activation(hwin[t][:, 0:M], ha[:], ACT.Copy, scale=0.5)
-                nc.scalar.activation(hpl[:, t, 0:M], ha[:], ACT.Copy, scale=0.5)
-                nc.scalar.activation(hwin[t][:, M:H], hb[:], ACT.Copy, scale=0.5)
-                nc.scalar.activation(hpl[:, t, M:H], hb[:], ACT.Copy, scale=0.5)
+                nc.scalar.activation(hwin[t][:, 0:256], h0[0][:], ACT.Copy, scale=0.5)
+                nc.scalar.activation(hpl[:, t, 0:256], h0[0][:], ACT.Copy, scale=0.5)
+                for c in (1, 2):
+                    nc.scalar.activation(hwin[t][:, CH[c][0] : CH[c][1]], h0[c][:], ACT.Copy, scale=0.5)
+                for c in (1, 2):
+                    nc.scalar.activation(hpl[:, t, CH[c][0] : CH[c][1]], h0[c][:], ACT.Copy, scale=0.5)
             else:
                 nc.scalar.activation(hwin[t][:], hs[t][:], ACT.Copy, scale=0.5)
                 nc.scalar.activation(hpl[:, t, 0:256], hs[t][:, 0:256], ACT.Copy, scale=0.5)
@@ -277,7 +312,7 @@ def tile_picked_tokstdtwice_none_po_kernel(
                 nc.vector.tensor_tensor(swin[t][:, a:b], hwin[t][:].indirect(lst(n3_t, a, b)), hpl[:, t, a:b], ALU.subtract)
             if t + 2 < 4:
                 hcopies(t + 2)
-        for a, b in ((0, 256), (256, 512)):
+        for a, b in CH:
             for t in range(4):
                 nc.scalar.activation(spl[:, t, a:b], swin[t][:, a:b], ACT.Copy, scale=2.0)
 

from contextlib import ExitStack

import concourse.mybir as mybir
from concourse.masks import make_identity

K, T, S, N, H = 512, 2048, 512, 512, 512
FLOPS = 2 * K * S * H + 2 * S * N * H

F32 = mybir.dt.float32
BF16 = mybir.dt.bfloat16
I32 = mybir.dt.int32
U32 = mybir.dt.uint32
U16 = mybir.dt.uint16
U8 = mybir.dt.uint8
FP8X4 = mybir.dt.float8_e4m3fn_x4
ALU = mybir.AluOpType
ACT = mybir.ActivationFunctionType

P = 128

CH = [(0, 256), (256, 384), (384, 512)]


def tile_picked_tokstdtwice_none_po_kernel(
    tc, x_words, x_scales, wa, gt, w1_words, w1_scales, offs, n1, n2, n3, out_0, out_1, out_2
):
    nc = tc.nc
    with ExitStack() as ctx:
        sb = ctx.enter_context(tc.tile_pool(name="sb", bufs=1))
        ps = ctx.enter_context(tc.psum_pool(name="ps", bufs=1))

        def tl(name, shape, dt, tag=None):
            return sb.tile(shape, dt, name=name, tag=tag or name, align_bytes=64)

        def lst(lt, a, b):
            return lt[:, a // 16 : b // 16]

        xs = tl("xs", [P, T], U8)
        nc.vector.memset(xs[:].bitcast(I32), 0)
        w1s = tl("w1s", [P, N], U8)
        nc.vector.memset(w1s[:].bitcast(I32), 0)
        sixteen = tl("sixteen", [P, 1], F32)
        nc.gpsimd.memset(sixteen[:], 16.0)
        quarter = tl("quarter", [P, 1], F32)
        nc.scalar.activation(quarter[:], sixteen[:], ACT.Abs_reciprocal_sqrt)

        ident = tl("ident", [P, P], F32)
        make_identity(nc, ident[:])

        offs_t = tl("offs_t", [P, S // 16], U16)
        n1_t = tl("n1_t", [P, H // 16], U16)
        n2_t = tl("n2_t", [P, H // 16], U16)
        n3_t = tl("n3_t", [P, H // 16], U16)
        for lt, src in ((offs_t, offs), (n1_t, n1), (n2_t, n2), (n3_t, n3)):
            nc.sync.dma_start(lt[:], src)
        xw = tl("xw", [P, T], U32)
        nc.sync.dma_start(xw[:].bitcast(I32), x_words[0].rearrange("p n t -> p (n t)").bitcast(I32))
        for q in range(4):
            nc.sync.dma_start(xs[32 * q : 32 * q + 4, :].bitcast(I32), x_scales[0, 4 * q : 4 * q + 4, :].bitcast(I32))
        wa_v = wa.rearrange("(p j) h -> p j h", j=4)
        wraw = []
        for c, (a, b) in enumerate(CH):
            w = tl(f"wraw{c}", [P, 4, b - a], F32)
            nc.sync.dma_start(w[:], wa_v[:, :, a:b])
            wraw.append(w)
        gt_t = tl("gt_t", [P, 4], F32)
        nc.sync.dma_start(gt_t[:], gt.rearrange("(p t) o -> p (t o)", t=4))
        w1w = tl("w1w", [P, N], U32)
        nc.sync.dma_start(w1w[:].bitcast(I32), w1_words[0].rearrange("p n t -> p (n t)").bitcast(I32))
        for q in range(4):
            nc.sync.dma_start(w1s[32 * q : 32 * q + 4, :].bitcast(I32), w1_scales[0, 4 * q : 4 * q + 4, :].bitcast(I32))

        def deal(dw, ds, words, scales, ta, tb):
            nc.vector.tensor_copy(
                dw[:].bitcast(I32).rearrange("p (t c i) -> p c t i", t=4, i=4)[:, :, ta:tb, :],
                words[:].bitcast(I32).rearrange("p (c i t) -> p c t i", t=4, i=4)[:, :, ta:tb, :],
            )
            nc.vector.tensor_copy(
                ds[:].rearrange("p (t c i) -> p c t i", t=4, i=16)[:, :, ta:tb, :],
                scales[:].rearrange("p (c i t) -> p c t i", t=4, i=16)[:, :, ta:tb, :],
            )

        xwg = tl("xwg", [P, S], U32)
        nc.vector.tensor_copy(xwg[:], xw[:].indirect(offs_t[:]))
        xsg = tl("xsg", [P, S], U8)
        nc.vector.tensor_copy(xsg[:], xs[:].indirect(offs_t[:]))
        xd = tl("xd", [P, S], U32)
        xds = tl("xds", [P, S], U8)
        deal(xd, xds, xwg, xsg, 0, 1)

        def interleave(eng, dst, src):
            o = dst[:].rearrange("p (c i) t -> p c t i", i=4)
            s = src.rearrange("p t (c i) -> p c t i", i=4)
            if eng == "v":
                nc.vector.tensor_copy(o, s)
            else:
                nc.scalar.copy(o, s)

        def quant(words, scales, src, a, b):
            nc.vector.quantize_mx(
                out=words[:, a:b].bitcast(FP8X4), scales=scales[:, a:b], in_=src[:].rearrange("p c t -> p (c t)")
            )

        def mm(out, lw, ls, t, rw, rs, a, b):
            nc.tensor.matmul_mx(
                out=out,
                lhsT=lw[:, P * t : P * (t + 1)].bitcast(FP8X4),
                lhsT_scale=ls[:, P * t : P * (t + 1)],
                rhs=rw[:, a:b].bitcast(FP8X4),
                rhs_scale=rs[:, a:b],
                start=True,
                stop=True,
            )

        gtc = tl("gtc", [P, 4], F32)
        nc.gpsimd.tensor_scalar(gtc[:], gt_t[:], -0.3125, 0.0, ALU.mult, ALU.add)

        waq = tl("waq", [P, H], U32)
        was = tl("was", [P, H], U8)
        y0 = [ps.tile([P, b - a], F32, name=f"y0{c}", tag=f"b{(0, 4, 5)[c]}") for c, (a, b) in enumerate(CH)]
        ys = [None] + [ps.tile([P, H], F32, name=f"y{t}", tag=f"b{t}") for t in range(1, 4)]
        for c, (a, b) in enumerate(CH):
            wb = tl(f"wb{c}", [P, b - a, 4], BF16)
            interleave("sss"[c], wb, wraw[c][:])
            quant(waq, was, wb, a, b)
            mm(y0[c][:], xd, xds, 0, waq, was, a, b)
        deal(xd, xds, xwg, xsg, 1, 2)
        deal(xd, xds, xwg, xsg, 2, 4)
        for t in range(1, 4):
            mm(ys[t][:], xd, xds, t, waq, was, 0, H)
        w1d = tl("w1d", [P, N], U32, tag=None)
        w1ds = tl("w1ds", [P, N], U8)
        gt6 = tl("gt6", [P, 4], F32)
        nc.gpsimd.tensor_scalar(gt6[:], gt_t[:], 1.0 / 6.0, 0.0, ALU.mult, ALU.add)
        FORM = "WWWWW"
        KS = {"T": -2.2, "W": -5.0 / 3.0}

        M = 384
        ywin = [tl(f"ywin{t}", [P, H], F32) for t in range(4)]
        yk = tl("yk", [P, 4, H], F32)
        yg = tl("yg", [P, 4, H], F32)
        A = [tl(f"A{t}", [P, M], F32) for t in range(4)]
        U = tl("U", [P, 4, H], F32)
        Eg = tl("Eg", [P, 4, H], F32)
        R = tl("R", [P, 4, H], F32)
        zq = tl("zq", [P, H], U32)
        zs = tl("zs", [P, H], U8)
        hwin = [tl(f"hwin{t}", [P, H], F32) for t in range(4)]
        hpl = tl("hpl", [P, 4, H], F32)

        def windows(t):
            if t == 0:
                for c, (a, b) in enumerate(CH):
                    nc.scalar.copy(ywin[t][:, a:b], y0[c][:])
                    if c < 2:
                        nc.vector.tensor_scalar(yk[:, t, a:b], ywin[t][:, a:b], KS[FORM[t]], None, ALU.mult)
                nc.scalar.activation(yk[:, t, M:H], y0[2][:], ACT.Copy, scale=KS[FORM[4]])
            else:
                nc.scalar.copy(ywin[t][:], ys[t][:])
                if FORM[t] == FORM[4]:
                    nc.scalar.activation(yk[:, t, :], ys[t][:], ACT.Copy, scale=KS[FORM[t]])
                else:
                    nc.scalar.activation(yk[:, t, 0:M], ys[t][:, 0:M], ACT.Copy, scale=KS[FORM[t]])
                    nc.scalar.activation(yk[:, t, M:H], ys[t][:, M:H], ACT.Copy, scale=KS[FORM[4]])

        def scaled(eng, dst, src, scale):
            if eng == "s":
                nc.scalar.activation(dst, src, ACT.Copy, scale=scale)
            else:
                nc.vector.tensor_scalar(dst, src, scale, None, ALU.mult)

        def aux(t, a, b, form, eng):
            if form == "W":
                scaled(eng, yg[:, t, a:b], ywin[t][:, a:b], gt6[:, t : t + 1])
            else:
                scaled(eng, yg[:, t, a:b], ywin[t][:, a:b], 8.0 / 15.0)

        def g1(t, a, b, dst):
            nc.vector.tensor_tensor(dst, ywin[t][:].indirect(lst(n1_t, a, b)), yk[:, t, a:b], ALU.add)

        def g2(t, a, b, k):
            nc.vector.tensor_tensor(U[:, t, a:b], ywin[t][:].indirect(lst(n2_t, a, b)), k, ALU.add)

        def tadd(out, terms):
            for i, x in enumerate(terms):
                nc.tensor.matmul(out, lhsT=x, rhs=ident[:], is_transpose=True, start=(i == 0), stop=(i == len(terms) - 1))

        st = {}

        def squares(n, a, u, k, k4, nb, form):
            X = tl(f"X{n}", [P, nb, P], F32)
            nc.vector.scalar_tensor_tensor(X[:], a, -2.0, u, ALU.mult, ALU.add)
            ut = ps.tile([P, nb, P], F32, name=f"ut{n}", tag=f"b{(6, 7, 4, 5, 7, 4)[n]}")
            vt = ps.tile([P, nb, P], F32, name=f"vt{n}", tag=f"b{(0, 1, 2, 3, 2, 3)[n]}")
            for j in range(nb):
                tadd(ut[:, j, :], [u[:, j, :]] if form == "W" else [u[:, j, :], k4[:, j, :]])
            for j in range(nb):
                tadd(vt[:, j, :], [X[:, j, :], k[:, j, :]])
            U2 = tl(f"U2{n}", [P, nb, P], F32)
            V2 = tl(f"V2{n}", [P, nb, P], F32)
            nc.scalar.activation(U2[:], ut[:], ACT.Square, scale=0.375)
            nc.scalar.activation(V2[:], vt[:], ACT.Square)
            st[n] = (U2, V2, nb)

        def root(n, dst):
            U2, V2, nb = st[n]
            d = ps.tile([P, nb, P], F32, name=f"d{n}", tag=f"b{(6, 7, 4, 5, 0, 1)[n]}")
            for j in range(nb):
                tadd(d[:, j, :], [V2[:, j, :], U2[:, j, :]])
            nc.scalar.activation(dst, d[:], ACT.Abs_reciprocal_sqrt, scale=0.5, bias=quarter[:])

        def blocks(ap):
            return ap.rearrange("p (j f) -> p j f", f=P)

        def finish(a, b):
            zb = tl(f"zb{a}", [P, b - a, 4], BF16)
            nc.vector.tensor_tensor(
                zb[:].rearrange("p (c i) t -> p c t i", i=4),
                Eg[:, :, a:b].rearrange("p t (c i) -> p c t i", i=4),
                R[:, :, a:b].rearrange("p t (c i) -> p c t i", i=4),
                ALU.mult,
            )
            return zb

        def gate(t, a, b, form, eng):
            if form == "W":
                nc.vector.scalar_tensor_tensor(Eg[:, t, a:b], U[:, t, a:b], gtc[:, t : t + 1], yg[:, t, a:b], ALU.mult, ALU.add)
            else:
                scaled(eng, Eg[:, t, a:b], U[:, t, a:b], gtc[:, t : t + 1])

        deal(w1d, w1ds, w1w, w1s, 0, 4)
        windows(0)
        for t in range(1, 4):
            windows(t)
        for t in range(4):
            if FORM[t] == "T":
                aux(t, 0, M, "T", "sssss"[t])
            g1(t, 0, 256, A[t][:, 0:256])
            g1(t, 256, M, A[t][:, 256:M])
            g2(t, 0, 256, A[t][:, 0:256])
            g2(t, 256, M, A[t][:, 256:M])
            if 4 <= t + 4 < 4 and t == 0:
                windows(3)
            squares(t, blocks(A[t][:]), blocks(U[:, t, 0:M]), blocks(yk[:, t, 0:M]), blocks(yg[:, t, 0:M]), 3, FORM[t])
            if t > 0:
                root(t - 1, blocks(R[:, t - 1, 0:M]))
            if FORM[t] == "W" and FORM[4] == "W":
                aux(t, 0, H, "W", "sssss"[t])
            else:
                if FORM[t] == "W":
                    aux(t, 0, M, "W", "sssss"[t])
                elif "vvvvv"[t] == "s":
                    gate(t, 0, M, "T", "s")
                aux(t, M, H, FORM[4], "sssss"[4])

        Al = tl("Al", [P, 4, P], F32, tag="A3")
        groups = [(0, 2), (2, 4)]
        g1(0, M, H, Al[:, 0, :])
        for t in range(4):
            if t < 3:
                g1(t + 1, M, H, Al[:, t + 1, :])
            g2(t, M, H, Al[:, t, :])
            if t == 0:
                root(3, blocks(R[:, 3, 0:M]))
            for u, (ta, tb) in enumerate(groups):
                if t == tb - 1:
                    squares(4 + u, Al[:, ta:tb, :], U[:, ta:tb, M:H], yk[:, ta:tb, M:H], yg[:, ta:tb, M:H], tb - ta, FORM[4])
                    if u > 0:
                        root(3 + u, R[:, groups[u - 1][0] : groups[u - 1][1], M:H])
        root(3 + len(groups), R[:, groups[-1][0] : groups[-1][1], M:H])
        for t in range(4):
            if t >= 4 and FORM[t] == FORM[4] and (FORM[t] == "W" or "vvvvv"[t] == "v"):
                gate(t, 0, H, FORM[t], "v")
            else:
                if FORM[t] == "W" or "vvvvv"[t] == "v":
                    gate(t, 0, M, FORM[t], "v")
                gate(t, M, H, FORM[4], "vvvvv"[4])
        h0 = [ps.tile([P, b - a], F32, name=f"h0{c}", tag=f"b{(2, 6, 4)[c]}") for c, (a, b) in enumerate(CH)]
        zb0 = finish(0, 256)
        zb1 = finish(256, M)
        quant(zq, zs, zb0, 0, 256)
        mm(h0[0][:], w1d, w1ds, 0, zq, zs, 0, 256)
        zb2 = finish(M, H)
        quant(zq, zs, zb1, 256, M)
        mm(h0[1][:], w1d, w1ds, 0, zq, zs, 256, M)
        quant(zq, zs, zb2, M, H)
        mm(h0[2][:], w1d, w1ds, 0, zq, zs, M, H)
        hs = [None] + [ps.tile([P, H], F32, name=f"h{t}", tag=f"b{(0, 7, 3, 5)[t]}") for t in range(1, 4)]
        for t in range(1, 4):
            mm(hs[t][:], w1d, w1ds, t, zq, zs, 0, H)

        swin = [tl(f"swin{t}", [P, H], F32) for t in range(4)]
        spl = tl("spl", [P, 4, H], F32)

        def hcopies(t):
            if t == 0:
                nc.scalar.activation(hwin[t][:, 0:256], h0[0][:], ACT.Copy, scale=0.5)
                nc.scalar.activation(hpl[:, t, 0:256], h0[0][:], ACT.Copy, scale=0.5)
                for c in (1, 2):
                    nc.scalar.activation(hwin[t][:, CH[c][0] : CH[c][1]], h0[c][:], ACT.Copy, scale=0.5)
                for c in (1, 2):
                    nc.scalar.activation(hpl[:, t, CH[c][0] : CH[c][1]], h0[c][:], ACT.Copy, scale=0.5)
            else:
                nc.scalar.activation(hwin[t][:], hs[t][:], ACT.Copy, scale=0.5)
                nc.scalar.activation(hpl[:, t, 0:256], hs[t][:, 0:256], ACT.Copy, scale=0.5)
                nc.scalar.activation(hpl[:, t, 256:H], hs[t][:, 256:H], ACT.Copy, scale=0.5)

        hcopies(0)
        hcopies(1)
        for t in range(4):
            for a, b in ((0, 256), (256, 512)):
                nc.vector.tensor_tensor(swin[t][:, a:b], hwin[t][:].indirect(lst(n3_t, a, b)), hpl[:, t, a:b], ALU.subtract)
            if t + 2 < 4:
                hcopies(t + 2)
        for a, b in CH:
            for t in range(4):
                nc.scalar.activation(spl[:, t, a:b], swin[t][:, a:b], ACT.Copy, scale=2.0)

        oq = tl("oq", [P, H], U32)
        osc = tl("osc", [P, H], U8)
        out_v = out_0.rearrange("(p t) h -> p t h", t=4)
        words_v = out_1[0].rearrange("p n t -> p (n t)").bitcast(I32)
        obs = []
        for c, (a, b) in enumerate(CH):
            O = tl(f"O{c}", [P, 4, b - a], F32)
            for t in range(4):
                nc.vector.tensor_tensor(O[:, t, :], swin[t][:].indirect(lst(n3_t, a, b)), spl[:, t, a:b], ALU.subtract)
            nc.sync.dma_start(out_v[:, :, a:b], O[:])
            ob = tl(f"ob{c}", [P, b - a, 4], BF16)
            interleave("s" if c < 2 else "v", ob, O[:])
            obs.append(ob)
        for c, (a, b) in enumerate(CH):
            quant(oq, osc, obs[c], a, b)
            nc.sync.dma_start(words_v[:, a:b], oq[:, a:b].bitcast(I32))
        for q in range(4):
            eng = nc.scalar if q % 2 == 0 else nc.sync
            eng.dma_start(out_2[0, 4 * q : 4 * q + 4, :].bitcast(I32), osc[32 * q : 32 * q + 4, :].bitcast(I32))
